import numpy as np
import ml_dtypes


def mxq(x, axis, fmt="e4m3"):
    dtype, down = {"e4m3": (ml_dtypes.float8_e4m3fn, 7), "e5m2": (ml_dtypes.float8_e5m2, 14)}[fmt]
    v = np.moveaxis(np.asarray(x, np.float32).astype(ml_dtypes.bfloat16).astype(np.float64), axis, -1)
    blocks = v.reshape(v.shape[:-1] + (-1, 32))
    amax = np.abs(blocks).max(-1, keepdims=True)
    byte = np.maximum(np.where(amax > 0, np.frexp(amax)[1] - 1 + 127, 0) - down, 1)
    scale = np.exp2(byte - 127.0)
    codes = (blocks / scale).astype(np.float32).astype(dtype).astype(np.float64)
    return np.moveaxis((codes * scale).reshape(v.shape), -1, axis)


WIDE = False


def mx_kscale(k):
    if not WIDE:
        return np.ones(k)
    levels = np.array([10, -10, 5, -5, 0])
    if k % 512:
        return np.exp2(np.random.permutation(np.resize(levels, k // 32))).repeat(32)
    a = np.empty((k // 512, 16))
    for p in range(k // 512):
        a[p, :8] = np.random.permutation(np.resize(levels, 8))
        for g in range(8):
            far = levels[np.abs(levels - a[p, g]) >= 10]
            a[p, g + 8] = far[np.random.randint(len(far))]
    return np.exp2(a.ravel()).repeat(32)


def f64(x):
    return np.asarray(x).astype(np.float64)


def striped(idx):
    return np.tile(np.asarray(idx).reshape(-1, 16).T, (8, 1)).astype(np.uint16)


def unstriped(offs):
    return offs[:16].T.reshape(-1).astype(np.int64)


def striped8(idx):
    return np.asarray(idx).reshape(8, -1, 16).transpose(0, 2, 1).reshape(128, -1).astype(np.uint16)


def unstriped8(offs):
    return offs.reshape(8, 16, -1).transpose(0, 2, 1).reshape(8, -1).astype(np.int64)


def pick8(x, idx, run):
    r = np.arange(len(x))
    return x[r[:, None], idx[r % (8 * run) // run]]


E2M1 = np.array([0.0, 0.5, 1.0, 1.5, 2.0, 3.0, 4.0, 6.0, -0.0, -0.5, -1.0, -1.5, -2.0, -3.0, -4.0, -6.0])


def pack_weight(w, fmt):
    k, n = w.shape
    w = f64(np.asarray(w, np.float32).astype(ml_dtypes.bfloat16)).reshape(k // 32, 32, n)
    amax = np.abs(w).max(1)
    if fmt == "e4m3":
        byte = np.frexp(amax)[1] - 1 + 127 - 7
    else:
        mant, ex = np.frexp(amax / 6.0)
        byte = np.where(mant > 0.5, ex, ex - 1) + 127
    byte = np.clip(np.where(amax > 0, byte, 1), 1, 254)
    scaled = (w * np.exp2(127.0 - byte)[:, None, :]).reshape(k, n).astype(np.float32)
    by_word = np.ascontiguousarray(scaled.reshape(k // 512, 128, 4, n).transpose(0, 1, 3, 2))
    if fmt == "e4m3":
        words = by_word.astype(ml_dtypes.float8_e4m3fn).view(np.uint8)
    else:
        c = by_word.astype(ml_dtypes.float4_e2m1fn).view(np.uint8) & 0xF
        words = (c[..., 0::2] | (c[..., 1::2] << 4)).reshape(k // 512, 128, 2 * n)
    return np.ascontiguousarray(words), np.ascontiguousarray(byte.astype(np.uint8).reshape(k // 512, 16, n))


def unpack_weight(words, scales, fmt):
    g, _, n = scales.shape
    words = np.ascontiguousarray(words).reshape(g, 128, n, -1)
    if fmt == "e4m3":
        vals = words.view(ml_dtypes.float8_e4m3fn).astype(np.float64)
    else:
        nib = np.empty((g, 128, n, 4), np.uint8)
        nib[..., 0::2] = words & 0xF
        nib[..., 1::2] = words >> 4
        vals = E2M1[nib]
    vals = vals * np.repeat(np.exp2(scales.astype(np.float64) - 127.0), 8, axis=1)[..., None]
    return vals.transpose(0, 1, 3, 2).reshape(g * 512, n)


K, J, R, T, F, Z, M, O, C, N, S, V = 512, 512, 512, 2048, 2048, 512, 1024, 256, 1024, 256, 512, 1024


def setup_inputs():
    n = np.random.standard_normal
    idx = np.random.permutation(T)[:J]
    idx2 = np.stack([np.random.permutation(F)[:R] for _ in range(8)])
    idx3 = np.random.permutation(M)[:J]
    idx4 = np.stack([np.random.permutation(C)[:J] for _ in range(8)])
    idx5 = np.stack([np.random.permutation(C)[:J] for _ in range(8)])
    idx6 = np.stack([np.random.permutation(J)[:O] for _ in range(8)])
    idx7 = np.random.permutation(V)[:O]
    fk = mx_kscale(K)
    fz = mx_kscale(Z)
    fr = mx_kscale(R)
    fs = mx_kscale(S)
    xtp = pack_weight(n((K, T)) * fk[:, None], "e4m3")
    xop = pack_weight(n((Z, M)) / fz[:, None], "e2m1")
    w2p = pack_weight(n((Z, R)) * 1 / np.sqrt(Z) * fz[:, None], "e4m3")
    wbp = pack_weight(n((R, N)) * 1 / np.sqrt(R) / fr[:, None], "e4m3")
    xrp = pack_weight(n((S, V)) / fs[:, None], "e2m1")
    wsp = pack_weight(n((S, N)) * 1 / np.sqrt(S) * fs[:, None], "e4m3")
    return {
        "xt_words": xtp[0],
        "xt_scales": xtp[1],
        "ua": (np.random.randint(-7, 8, (K, F)).astype(np.float64)).astype(np.float32),
        "ha": ((np.random.randint(8, 25, (K, 1)) / 1024.0) / fk[:, None]).astype(np.float32),
        "xo_words": xop[0],
        "xo_scales": xop[1],
        "w2_words": w2p[0],
        "w2_scales": w2p[1],
        "sa": (np.random.uniform(0.5, 1.6, (R, 1))).astype(np.float32),
        "sb": (np.random.uniform(0.5, 1.6, (R, 1)) * fr[:, None]).astype(np.float32),
        "wb_words": wbp[0],
        "wb_scales": wbp[1],
        "xr_words": xrp[0],
        "xr_scales": xrp[1],
        "ws_words": wsp[0],
        "ws_scales": wsp[1],
        "offs": striped(idx),
        "offs2": striped8(idx2),
        "offs3": striped(idx3),
        "offs4": striped8(idx4),
        "offs5": striped8(idx5),
        "offs6": striped8(idx6),
        "offs7": striped(idx7),
    }


def reference(xt_words, xt_scales, ua, ha, xo_words, xo_scales, w2_words, w2_scales, sa, sb, wb_words, wb_scales, xr_words, xr_scales, ws_words, ws_scales, offs, offs2, offs3, offs4, offs5, offs6, offs7):
    idx = unstriped(offs)
    idx2 = unstriped8(offs2)
    idx3 = unstriped(offs3)
    idx4 = unstriped8(offs4)
    idx5 = unstriped8(offs5)
    idx6 = unstriped8(offs6)
    idx7 = unstriped(offs7)
    xtu = unpack_weight(xt_words, xt_scales, "e4m3")
    xou = unpack_weight(xo_words, xo_scales, "e2m1")
    w2u = unpack_weight(w2_words, w2_scales, "e4m3")
    wbu = unpack_weight(wb_words, wb_scales, "e4m3")
    xru = unpack_weight(xr_words, xr_scales, "e2m1")
    wsu = unpack_weight(ws_words, ws_scales, "e4m3")
    wc = pick8(f64(ua), idx2, 64) * f64(ha)
    wcq = mxq(wc, 0, "e4m3")
    xtidxg = xtu[:, idx]
    a = wcq.T @ xtidxg
    xoidx3g = xou[:, idx3]
    b = w2u.T @ xoidx3g
    pw = np.zeros((R, C))
    pw[np.arange(R)[:, None], idx4[np.arange(R) % 512 // 64]] = a
    g1 = np.maximum(pick8(pw, idx5, 64) * f64(sa), b)
    hid = pick8(g1, idx6, 64) * f64(sb)
    hidq = mxq(hid, 0, "e4m3")
    xridx7g = xru[:, idx7]
    y = wbu.T @ hidq + wsu.T @ xridx7g
    return y

@@ -1,0 +1,255 @@
+from contextlib import ExitStack
+
+import concourse.mybir as mybir
+
+K, J, R, T, F, Z, M, O, C, N, S, V = 512, 512, 512, 2048, 2048, 512, 1024, 256, 1024, 256, 512, 1024
+FLOPS = 2 * K * R * J + 2 * Z * R * J + 2 * R * N * O + 2 * S * N * O
+
+F32 = mybir.dt.float32
+BF16 = mybir.dt.bfloat16
+I32 = mybir.dt.int32
+U32 = mybir.dt.uint32
+U16 = mybir.dt.uint16
+U8 = mybir.dt.uint8
+FP8X4 = mybir.dt.float8_e4m3fn_x4
+FP4X4 = mybir.dt.float4_e2m1fn_x4
+COPY = mybir.ActivationFunctionType.Copy
+MAX = mybir.AluOpType.max
+
+P = 128
+PACK = 4
+LANES = 16
+XT_ROW = 4
+
+
+def tile_picked_tokens_codes_two_answered_reminder_plain_kernel(
+    tc, xt_words, xt_scales, ua, ha, xo_words, xo_scales, w2_words, w2_scales, sa, sb,
+    wb_words, wb_scales, xr_words, xr_scales, ws_words, ws_scales,
+    offs, offs2, offs3, offs4, offs5, offs6, offs7, out,
+):
+    nc = tc.nc
+    with ExitStack() as ctx:
+        lists = ctx.enter_context(tc.tile_pool(name="lists", bufs=1))
+        keep = ctx.enter_context(tc.tile_pool(name="keep", bufs=1))
+        psum = ctx.enter_context(tc.psum_pool(name="psum", bufs=1))
+
+        def load_list(src, name):
+            t = lists.tile(list(src.shape), U16, name=name)
+            nc.sync.dma_start(t[:], src)
+            return t
+
+        def load_column(src, name):
+            t = keep.tile([P, PACK], F32, name=name)
+            nc.sync.dma_start(t[:], src.rearrange("(p t) o -> p (t o)", t=PACK))
+            return t
+
+        def load_words8(src, cols, name):
+            t = keep.tile([P, cols], U32, name=name, align_bytes=64)
+            nc.sync.dma_start(t[:].bitcast(I32), src[0].rearrange("p n t -> p (n t)").bitcast(I32))
+            return t
+
+        def load_words4(src, cols, name):
+            t = keep.tile([P, cols], U16, name=name, align_bytes=64)
+            nc.sync.dma_start(t[:].bitcast(I32), src[0].bitcast(I32))
+            return t
+
+        def cleared_plane(cols, name):
+            t = keep.tile([P, cols], U8, name=name, align_bytes=64)
+            nc.vector.memset(t[:].bitcast(I32), 0)
+            return t
+
+        def load_plane(plane, src, row):
+            for q in range(4):
+                nc.sync.dma_start(plane[32 * q + row : 32 * q + row + 4, :].bitcast(I32),
+                                  src[0, 4 * q : 4 * q + 4, :].bitcast(I32))
+
+        def load_staged(src, cols, name):
+            t = keep.tile([P, 2, cols // 4], I32, name=name)
+            for h in range(2):
+                nc.sync.dma_start(t[64 * h : 64 * h + 4, :, :],
+                                  src[0, 8 * h : 8 * h + 8, :].bitcast(I32).rearrange("(q r) n -> r q n", q=2))
+            return t
+
+        def spread(plane, staged):
+            for q in range(4):
+                nc.vector.tensor_copy(plane[32 * q : 32 * q + 4, :].bitcast(I32),
+                                      staged[64 * (q // 2) : 64 * (q // 2) + 4, q % 2, :])
+
+        xt_plane = cleared_plane(T, "xt_plane")
+        xo_plane = cleared_plane(M, "xo_plane")
+        w2_plane = cleared_plane(R, "w2_plane")
+        boards = []
+        for t in range(PACK):
+            board = keep.tile([P, C], F32, name="board%d" % t)
+            nc.gpsimd.memset(board[:], 0.0)
+            boards.append(board)
+        xr_plane = cleared_plane(V, "xr_plane")
+        wb_plane = cleared_plane(N, "wb_plane")
+        ws_plane = cleared_plane(N, "ws_plane")
+
+        ua_rows = ua.rearrange("(p t) f -> p t f", t=PACK)
+        tables = [keep.tile([P, F], F32, name="table%d" % t) for t in range(PACK)]
+        nc.sync.dma_start(tables[0][:], ua_rows[:, 0, :])
+        l2 = load_list(offs2, "l2")
+        ha_t = load_column(ha, "ha_t")
+        l3 = load_list(offs3, "l3")
+        xo_staged = load_staged(xo_scales, M, "xo_staged")
+        l1 = load_list(offs, "l1")
+        nc.sync.dma_start(tables[1][:], ua_rows[:, 1, :])
+        load_plane(xt_plane, xt_scales, XT_ROW)
+        nc.sync.dma_start(tables[2][:], ua_rows[:, 2, :])
+        w2_staged = load_staged(w2_scales, R, "w2_staged")
+        xr_staged = load_staged(xr_scales, V, "xr_staged")
+        l7 = load_list(offs7, "l7")
+        nc.sync.dma_start(tables[3][:], ua_rows[:, 3, :])
+        xo_table = load_words4(xo_words, M, "xo_table")
+        xt_table = load_words8(xt_words, T, "xt_table")
+        l4 = load_list(offs4, "l4")
+        xr_table = load_words4(xr_words, V, "xr_table")
+        w2_raw = load_words8(w2_words, R, "w2_raw")
+        l5 = load_list(offs5, "l5")
+        sa_t = load_column(sa, "sa_t")
+        l6 = load_list(offs6, "l6")
+        sb_t = load_column(sb, "sb_t")
+        ws_codes = load_words8(ws_words, N, "ws_codes")
+        load_plane(ws_plane, ws_scales, 0)
+        wb_codes = load_words8(wb_words, N, "wb_codes")
+        load_plane(wb_plane, wb_scales, 0)
+
+        wc_planes = keep.tile([P, PACK, R], BF16, name="wc_planes")
+        for t in range(PACK):
+            nc.scalar.activation(wc_planes[:, t, :], tables[t][:].indirect(l2[:]), COPY, scale=ha_t[:, t : t + 1])
+        spread(xo_plane, xo_staged)
+        xo_sc = keep.tile([P, J], U8, name="xo_sc", align_bytes=64)
+        nc.vector.tensor_copy(xo_sc[:], xo_plane[:].indirect(l3[:]))
+        xt_sc = keep.tile([P, J], U8, name="xt_sc", align_bytes=64)
+        nc.vector.tensor_copy(xt_sc[:], xt_plane[:].indirect(l1[:]))
+        spread(w2_plane, w2_staged)
+        w2_sc = keep.tile([P, R], U8, name="w2_sc", align_bytes=64)
+        nc.vector.tensor_copy(w2_sc[:].rearrange("p (u m) -> p u m", u=PACK),
+                              w2_plane[:].rearrange("p (m u) -> p u m", u=PACK))
+        spread(xr_plane, xr_staged)
+        xr_sc = keep.tile([P, O], U8, name="xr_sc", align_bytes=64)
+        nc.vector.tensor_copy(xr_sc[:], xr_plane[:].indirect(l7[:]))
+        xo_codes = keep.tile([P, J], U16, name="xo_codes", align_bytes=64)
+        nc.vector.tensor_copy(xo_codes[:], xo_table[:].indirect(l3[:]))
+
+        wc_dealt = wc_planes[:].rearrange("p t (m u) -> p u m t", u=PACK)
+        wc_in0 = keep.tile([P, P, PACK], BF16, name="wc_in0", align_bytes=64)
+        wc_in1 = keep.tile([P, P, PACK], BF16, name="wc_in1", align_bytes=64)
+        wc_in23 = keep.tile([P, 2, P, PACK], BF16, name="wc_in23", align_bytes=64)
+        wc_codes = [keep.tile([P, w * P], U32, name="wc_codes%d" % i, align_bytes=64) for i, w in enumerate((1, 1, 2))]
+        wc_sc = [keep.tile([P, w * P], U8, name="wc_sc%d" % i, align_bytes=64) for i, w in enumerate((1, 1, 2))]
+
+        nc.vector.tensor_copy(wc_in0[:], wc_dealt[:, 0])
+        nc.scalar.copy(wc_in1[:], wc_dealt[:, 1])
+        nc.vector.quantize_mx(wc_codes[0][:].bitcast(FP8X4), wc_sc[0][:], wc_in0[:].rearrange("p m t -> p (m t)"))
+
+        xt_codes = [keep.tile([P, J // 2], U32, name="xt_codes%d" % h, align_bytes=64) for h in range(2)]
+        HJ = J // 2
+        for h in range(2):
+            nc.vector.tensor_copy(xt_codes[h][:], xt_table[:].indirect(l1[:, h * HJ // LANES : (h + 1) * HJ // LANES]))
+        xr_codes = keep.tile([P, O], U16, name="xr_codes", align_bytes=64)
+        nc.vector.tensor_copy(xr_codes[:], xr_table[:].indirect(l7[:]))
+
+        def first_product(bank, u, h):
+            i, c = min(u, 2), max(u - 2, 0) * P
+            nc.tensor.matmul_mx(bank, lhsT=wc_codes[i][:, c : c + P].bitcast(FP8X4), lhsT_scale=wc_sc[i][:, c : c + P],
+                                rhs=xt_codes[h][:].bitcast(FP8X4), rhs_scale=xt_sc[XT_ROW:P, h * HJ : (h + 1) * HJ],
+                                start=True, stop=True)
+
+        a_sb = [keep.tile([P, J], F32, name="a_sb%d" % u) for u in range(PACK)]
+        for h in range(2):
+            bank = psum.tile([P, J], F32, name="a_bank", tag="a_bank", bufs=3)
+            first_product(bank[:, 0:HJ], 0, h)
+            nc.scalar.copy(a_sb[0][:, h * HJ : (h + 1) * HJ], bank[:, 0:HJ])
+        nc.vector.tensor_copy(boards[0][:].indirect(l4[:, 0 : HJ // LANES]), a_sb[0][:, 0:HJ])
+        nc.vector.quantize_mx(wc_codes[1][:].bitcast(FP8X4), wc_sc[1][:], wc_in1[:].rearrange("p m t -> p (m t)"))
+        nc.vector.tensor_copy(boards[0][:].indirect(l4[:, HJ // LANES : J // LANES]), a_sb[0][:, HJ:J])
+
+        def product_a(u):
+            bank = psum.tile([P, J], F32, name="a_bank", tag="a_bank", bufs=3)
+            for h in range(2):
+                first_product(bank[:, h * HJ : (h + 1) * HJ], u, h)
+            nc.scalar.copy(a_sb[u][:], bank[:])
+
+        def scatter(u):
+            nc.vector.tensor_copy(boards[u][:].indirect(l4[:]), a_sb[u][:])
+
+        product_a(1)
+        for u in range(2):
+            nc.scalar.copy(wc_in23[:, u], wc_dealt[:, 2 + u])
+        nc.vector.quantize_mx(wc_codes[2][:].bitcast(FP8X4), wc_sc[2][:], wc_in23[:].rearrange("p u m t -> p (u m t)"))
+        w2_codes = keep.tile([P, R], U32, name="w2_codes", align_bytes=64)
+        nc.scalar.copy(w2_codes[:].rearrange("p (u m) -> p u m", u=PACK), w2_raw[:].rearrange("p (m u) -> p u m", u=PACK))
+        scatter(1)
+
+        b_banks = {}
+
+        def product_b(u):
+            b_banks[u] = psum.tile([P, J], F32, name="b_bank", tag="b_bank", bufs=3)
+            nc.tensor.matmul_mx(b_banks[u][:], lhsT=w2_codes[:, u * P : (u + 1) * P].bitcast(FP8X4),
+                                lhsT_scale=w2_sc[:, u * P : (u + 1) * P], rhs=xo_codes[:].bitcast(FP4X4),
+                                rhs_scale=xo_sc[:], start=True, stop=True)
+
+        read = [keep.tile([P, J], F32, name="read%d" % u) for u in range(PACK)]
+        g1 = [keep.tile([P, J], F32, name="g1_%d" % u) for u in range(PACK)]
+        hid_planes = keep.tile([P, PACK, O], BF16, name="hid_planes")
+
+        def read_board(u, lo, hi):
+            nc.scalar.activation(read[u][:, lo:hi], boards[u][:].indirect(l5[:, lo // LANES : hi // LANES]), COPY,
+                                 scale=sa_t[:, u : u + 1])
+
+        def larger(u, lo, hi):
+            nc.vector.tensor_tensor(g1[u][:, lo:hi], read[u][:, lo:hi], b_banks[u][:, lo:hi], MAX)
+
+        def answers(u, lo, hi):
+            nc.scalar.activation(hid_planes[:, u, lo:hi], g1[u][:].indirect(l6[:, lo // LANES : hi // LANES]), COPY,
+                                 scale=sb_t[:, u : u + 1])
+
+        product_b(0)
+        read_board(0, 0, J)
+        product_a(2)
+        product_b(1)
+        larger(0, 0, J)
+        scatter(2)
+        read_board(1, 0, J)
+        product_a(3)
+        product_b(2)
+        answers(0, 0, O)
+        larger(1, 0, J)
+        scatter(3)
+        product_b(3)
+        read_board(2, 0, J)
+        answers(1, 0, O)
+        larger(2, 0, J)
+        read_board(3, 0, HJ)
+        read_board(3, HJ, J)
+
+        larger(3, 0, HJ)
+        answers(2, 0, O)
+        larger(3, HJ, J)
+        out_banks = [psum.tile([P, O], F32, name="out_bank%d" % n) for n in range(2)]
+        for n in range(2):
+            nc.tensor.matmul_mx(out_banks[n][:], lhsT=ws_codes[:, n * P : (n + 1) * P].bitcast(FP8X4),
+                                lhsT_scale=ws_plane[:, n * P : (n + 1) * P], rhs=xr_codes[:].bitcast(FP4X4),
+                                rhs_scale=xr_sc[:], start=True, stop=False)
+        HO = O // 2
+        hid_in = [keep.tile([P, HO, PACK], BF16, name="hid_in%d" % h, align_bytes=64) for h in range(2)]
+        hid_codes = [keep.tile([P, HO], U32, name="hid_codes%d" % h, align_bytes=64) for h in range(2)]
+        hid_sc = [keep.tile([P, HO], U8, name="hid_sc%d" % h, align_bytes=64) for h in range(2)]
+        for h in range(2):
+            answers(3, h * HO, (h + 1) * HO)
+        for h in range(2):
+            nc.vector.tensor_copy(hid_in[h][:], hid_planes[:, :, h * HO : (h + 1) * HO].rearrange("p t o -> p o t"))
+        for h in range(2):
+            nc.vector.quantize_mx(hid_codes[h][:].bitcast(FP8X4), hid_sc[h][:], hid_in[h][:].rearrange("p o t -> p (o t)"))
+            for n in range(2):
+                nc.tensor.matmul_mx(out_banks[n][:, h * HO : (h + 1) * HO], lhsT=wb_codes[:, n * P : (n + 1) * P].bitcast(FP8X4),
+                                    lhsT_scale=wb_plane[:, n * P : (n + 1) * P], rhs=hid_codes[h][:].bitcast(FP8X4),
+                                    rhs_scale=hid_sc[h][:], start=False, stop=(h == 1))
+        result = [keep.tile([P, O], F32, name="result%d" % n) for n in range(2)]
+        nc.scalar.copy(result[0][:], out_banks[0][:])
+        nc.scalar.dma_start(out[0:P, :], result[0][:])
+        nc.vector.tensor_copy(result[1][:], out_banks[1][:])
+        nc.sync.dma_start(out[P : 2 * P, :], result[1][:])

@@ -44,7 +44,7 @@ def tile_picked_tokens_codes_two_answered_reminder_plain_kernel(
             return t
 
         def load_words8(src, cols, name):
-            t = keep.tile([P, cols], U32, name=name, align_bytes=64)
+            t = keep.tile([P, cols], U32, name=name, tag=name, align_bytes=64)
             nc.sync.dma_start(t[:].bitcast(I32), src[0].rearrange("p n t -> p (n t)").bitcast(I32))
             return t
 
@@ -53,20 +53,20 @@ def tile_picked_tokens_codes_two_answered_reminder_plain_kernel(
             nc.sync.dma_start(t[:].bitcast(I32), src[0].bitcast(I32))
             return t
 
-        def cleared_plane(cols, name):
-            t = keep.tile([P, cols], U8, name=name, align_bytes=64)
+        def cleared_plane(cols, name, tag):
+            t = keep.tile([P, cols], U8, name=name, tag=tag, align_bytes=64)
             nc.vector.memset(t[:].bitcast(I32), 0)
             return t
 
         def load_plane(plane, src, row):
-            for q in range(4):
-                nc.sync.dma_start(plane[32 * q + row : 32 * q + row + 4, :].bitcast(I32),
-                                  src[0, 4 * q : 4 * q + 4, :].bitcast(I32))
+            rows = src[0].bitcast(I32).rearrange("(q r) n -> r q n", r=4)
+            for r in range(4):
+                nc.sync.dma_start(plane[row + r : P : 32, :].bitcast(I32), rows[r])
 
-        def load_staged(src, cols, name):
-            t = keep.tile([P, 2, cols // 4], I32, name=name)
+        def load_staged(src, cols, name, queue):
+            t = keep.tile([P, 2, cols // 4], I32, name=name, tag=name, align_bytes=64)
             for h in range(2):
-                nc.sync.dma_start(t[64 * h : 64 * h + 4, :, :],
+                queue.dma_start(t[64 * h : 64 * h + 4, :, :],
                                   src[0, 8 * h : 8 * h + 8, :].bitcast(I32).rearrange("(q r) n -> r q n", q=2))
             return t
 
@@ -75,17 +75,19 @@ def tile_picked_tokens_codes_two_answered_reminder_plain_kernel(
                 nc.vector.tensor_copy(plane[32 * q : 32 * q + 4, :].bitcast(I32),
                                       staged[64 * (q // 2) : 64 * (q // 2) + 4, q % 2, :])
 
-        xt_plane = cleared_plane(T, "xt_plane")
-        xo_plane = cleared_plane(M, "xo_plane")
-        w2_plane = cleared_plane(R, "w2_plane")
+        w2_staged = load_staged(w2_scales, R, "w2_staged", nc.gpsimd)
+        xo_staged = load_staged(xo_scales, M, "xo_staged", nc.gpsimd)
+        xt_plane = cleared_plane(T, "xt_plane", "xt_plane")
+        w2_plane = cleared_plane(R, "w2_plane", "w2_plane")
+        xo_plane = cleared_plane(M, "xo_plane", "xo_plane")
         boards = []
         for t in range(PACK):
             board = keep.tile([P, C], F32, name="board%d" % t)
             nc.gpsimd.memset(board[:], 0.0)
             boards.append(board)
-        xr_plane = cleared_plane(V, "xr_plane")
-        wb_plane = cleared_plane(N, "wb_plane")
-        ws_plane = cleared_plane(N, "ws_plane")
+        xr_plane = cleared_plane(V, "xr_plane", "xr_plane")
+        wb_plane = cleared_plane(N, "wb_plane", "wb_plane")
+        ws_plane = cleared_plane(N, "ws_plane", "ws_plane")
 
         ua_rows = ua.rearrange("(p t) f -> p t f", t=PACK)
         tables = [keep.tile([P, F], F32, name="table%d" % t) for t in range(PACK)]
@@ -93,24 +95,22 @@ def tile_picked_tokens_codes_two_answered_reminder_plain_kernel(
         l2 = load_list(offs2, "l2")
         ha_t = load_column(ha, "ha_t")
         l3 = load_list(offs3, "l3")
-        xo_staged = load_staged(xo_scales, M, "xo_staged")
         l1 = load_list(offs, "l1")
         nc.sync.dma_start(tables[1][:], ua_rows[:, 1, :])
-        load_plane(xt_plane, xt_scales, XT_ROW)
         nc.sync.dma_start(tables[2][:], ua_rows[:, 2, :])
-        w2_staged = load_staged(w2_scales, R, "w2_staged")
-        xr_staged = load_staged(xr_scales, V, "xr_staged")
-        l7 = load_list(offs7, "l7")
+        load_plane(xt_plane, xt_scales, XT_ROW)
         nc.sync.dma_start(tables[3][:], ua_rows[:, 3, :])
         xo_table = load_words4(xo_words, M, "xo_table")
         xt_table = load_words8(xt_words, T, "xt_table")
         l4 = load_list(offs4, "l4")
-        xr_table = load_words4(xr_words, V, "xr_table")
         w2_raw = load_words8(w2_words, R, "w2_raw")
         l5 = load_list(offs5, "l5")
         sa_t = load_column(sa, "sa_t")
         l6 = load_list(offs6, "l6")
         sb_t = load_column(sb, "sb_t")
+        l7 = load_list(offs7, "l7")
+        xr_table = load_words4(xr_words, V, "xr_table")
+        load_plane(xr_plane, xr_scales, 0)
         ws_codes = load_words8(ws_words, N, "ws_codes")
         load_plane(ws_plane, ws_scales, 0)
         wb_codes = load_words8(wb_words, N, "wb_codes")
@@ -119,52 +119,46 @@ def tile_picked_tokens_codes_two_answered_reminder_plain_kernel(
         wc_planes = keep.tile([P, PACK, R], BF16, name="wc_planes")
         for t in range(PACK):
             nc.scalar.activation(wc_planes[:, t, :], tables[t][:].indirect(l2[:]), COPY, scale=ha_t[:, t : t + 1])
+        spread(w2_plane, w2_staged)
+        w2_sc = keep.tile([P, R], U8, name="w2_sc", align_bytes=64)
+        nc.vector.tensor_copy(w2_sc[:].rearrange("p (u m) -> p u m", u=PACK),
+                              w2_plane[:].rearrange("p (m u) -> p u m", u=PACK))
         spread(xo_plane, xo_staged)
         xo_sc = keep.tile([P, J], U8, name="xo_sc", align_bytes=64)
         nc.vector.tensor_copy(xo_sc[:], xo_plane[:].indirect(l3[:]))
         xt_sc = keep.tile([P, J], U8, name="xt_sc", align_bytes=64)
         nc.vector.tensor_copy(xt_sc[:], xt_plane[:].indirect(l1[:]))
-        spread(w2_plane, w2_staged)
-        w2_sc = keep.tile([P, R], U8, name="w2_sc", align_bytes=64)
-        nc.vector.tensor_copy(w2_sc[:].rearrange("p (u m) -> p u m", u=PACK),
-                              w2_plane[:].rearrange("p (m u) -> p u m", u=PACK))
-        spread(xr_plane, xr_staged)
-        xr_sc = keep.tile([P, O], U8, name="xr_sc", align_bytes=64)
-        nc.vector.tensor_copy(xr_sc[:], xr_plane[:].indirect(l7[:]))
         xo_codes = keep.tile([P, J], U16, name="xo_codes", align_bytes=64)
         nc.vector.tensor_copy(xo_codes[:], xo_table[:].indirect(l3[:]))
 
         wc_dealt = wc_planes[:].rearrange("p t (m u) -> p u m t", u=PACK)
-        wc_in0 = keep.tile([P, P, PACK], BF16, name="wc_in0", align_bytes=64)
-        wc_in1 = keep.tile([P, P, PACK], BF16, name="wc_in1", align_bytes=64)
-        wc_in23 = keep.tile([P, 2, P, PACK], BF16, name="wc_in23", align_bytes=64)
-        wc_codes = [keep.tile([P, w * P], U32, name="wc_codes%d" % i, align_bytes=64) for i, w in enumerate((1, 1, 2))]
-        wc_sc = [keep.tile([P, w * P], U8, name="wc_sc%d" % i, align_bytes=64) for i, w in enumerate((1, 1, 2))]
-
-        nc.vector.tensor_copy(wc_in0[:], wc_dealt[:, 0])
-        nc.scalar.copy(wc_in1[:], wc_dealt[:, 1])
-        nc.vector.quantize_mx(wc_codes[0][:].bitcast(FP8X4), wc_sc[0][:], wc_in0[:].rearrange("p m t -> p (m t)"))
+        wc_in = [keep.tile([P, w, P, PACK], BF16, name="wc_in%d" % w, align_bytes=64) for w in (1, 3)]
+        wc_sc = [keep.tile([P, w * P], U8, name="wc_sc%d" % w, align_bytes=64) for w in (1, 3)]
+        wc_codes = [keep.tile([P, P], U32, name="wc_codes_first", align_bytes=64)]
+        nc.vector.tensor_copy(wc_in[0][:, 0], wc_dealt[:, 0])
+        for u in range(1, PACK):
+            nc.scalar.copy(wc_in[1][:, u - 1], wc_dealt[:, u])
+        nc.vector.quantize_mx(wc_codes[0][:].bitcast(FP8X4), wc_sc[0][:], wc_in[0][:].rearrange("p u m t -> p (u m t)"))
 
         xt_codes = [keep.tile([P, J // 2], U32, name="xt_codes%d" % h, align_bytes=64) for h in range(2)]
         HJ = J // 2
         for h in range(2):
             nc.vector.tensor_copy(xt_codes[h][:], xt_table[:].indirect(l1[:, h * HJ // LANES : (h + 1) * HJ // LANES]))
-        xr_codes = keep.tile([P, O], U16, name="xr_codes", align_bytes=64)
-        nc.vector.tensor_copy(xr_codes[:], xr_table[:].indirect(l7[:]))
+        wc_codes.append(keep.tile([P, 3 * P], U32, name="wc_codes_rest", tag="xt_table", align_bytes=64))
+        nc.vector.quantize_mx(wc_codes[1][:].bitcast(FP8X4), wc_sc[1][:], wc_in[1][:].rearrange("p u m t -> p (u m t)"))
 
         def first_product(bank, u, h):
-            i, c = min(u, 2), max(u - 2, 0) * P
+            i, c = min(u, 1), max(u - 1, 0) * P
             nc.tensor.matmul_mx(bank, lhsT=wc_codes[i][:, c : c + P].bitcast(FP8X4), lhsT_scale=wc_sc[i][:, c : c + P],
                                 rhs=xt_codes[h][:].bitcast(FP8X4), rhs_scale=xt_sc[XT_ROW:P, h * HJ : (h + 1) * HJ],
                                 start=True, stop=True)
 
-        a_sb = [keep.tile([P, J], F32, name="a_sb%d" % u) for u in range(PACK)]
+        a_sb = [keep.tile([P, J], F32, name="a_sb%d" % u, tag="a_sb%d" % u, align_bytes=64) for u in range(PACK)]
         for h in range(2):
             bank = psum.tile([P, J], F32, name="a_bank", tag="a_bank", bufs=3)
             first_product(bank[:, 0:HJ], 0, h)
             nc.scalar.copy(a_sb[0][:, h * HJ : (h + 1) * HJ], bank[:, 0:HJ])
         nc.vector.tensor_copy(boards[0][:].indirect(l4[:, 0 : HJ // LANES]), a_sb[0][:, 0:HJ])
-        nc.vector.quantize_mx(wc_codes[1][:].bitcast(FP8X4), wc_sc[1][:], wc_in1[:].rearrange("p m t -> p (m t)"))
         nc.vector.tensor_copy(boards[0][:].indirect(l4[:, HJ // LANES : J // LANES]), a_sb[0][:, HJ:J])
 
         def product_a(u):
@@ -177,11 +171,8 @@ def tile_picked_tokens_codes_two_answered_reminder_plain_kernel(
             nc.vector.tensor_copy(boards[u][:].indirect(l4[:]), a_sb[u][:])
 
         product_a(1)
-        for u in range(2):
-            nc.scalar.copy(wc_in23[:, u], wc_dealt[:, 2 + u])
-        nc.vector.quantize_mx(wc_codes[2][:].bitcast(FP8X4), wc_sc[2][:], wc_in23[:].rearrange("p u m t -> p (u m t)"))
         w2_codes = keep.tile([P, R], U32, name="w2_codes", align_bytes=64)
-        nc.scalar.copy(w2_codes[:].rearrange("p (u m) -> p u m", u=PACK), w2_raw[:].rearrange("p (m u) -> p u m", u=PACK))
+        nc.scalar.copy(w2_codes[:].rearrange("p (u m) -> p m u", u=PACK), w2_raw[:].rearrange("p (m u) -> p m u", u=PACK))
         scatter(1)
 
         b_banks = {}
@@ -192,8 +183,8 @@ def tile_picked_tokens_codes_two_answered_reminder_plain_kernel(
                                 lhsT_scale=w2_sc[:, u * P : (u + 1) * P], rhs=xo_codes[:].bitcast(FP4X4),
                                 rhs_scale=xo_sc[:], start=True, stop=True)
 
-        read = [keep.tile([P, J], F32, name="read%d" % u) for u in range(PACK)]
-        g1 = [keep.tile([P, J], F32, name="g1_%d" % u) for u in range(PACK)]
+        read = [keep.tile([P, J], F32, name="read%d" % u, tag="read%d" % u, align_bytes=64) for u in range(PACK)]
+        g1 = {}
         hid_planes = keep.tile([P, PACK, O], BF16, name="hid_planes")
 
         def read_board(u, lo, hi):
@@ -201,6 +192,8 @@ def tile_picked_tokens_codes_two_answered_reminder_plain_kernel(
                                  scale=sa_t[:, u : u + 1])
 
         def larger(u, lo, hi):
+            if lo == 0:
+                g1[u] = keep.tile([P, J], F32, name="g1_%d" % u, tag="a_sb%d" % ((u + 1) % PACK), align_bytes=64)
             nc.vector.tensor_tensor(g1[u][:, lo:hi], read[u][:, lo:hi], b_banks[u][:, lo:hi], MAX)
 
         def answers(u, lo, hi):
@@ -223,12 +216,13 @@ def tile_picked_tokens_codes_two_answered_reminder_plain_kernel(
         read_board(2, 0, J)
         answers(1, 0, O)
         larger(2, 0, J)
-        read_board(3, 0, HJ)
-        read_board(3, HJ, J)
-
-        larger(3, 0, HJ)
+        xr_sc = keep.tile([P, O], U8, name="xr_sc", tag="read2", align_bytes=64)
+        nc.vector.tensor_copy(xr_sc[:], xr_plane[:].indirect(l7[:]))
+        read_board(3, 0, J)
         answers(2, 0, O)
-        larger(3, HJ, J)
+        larger(3, 0, J)
+        xr_codes = keep.tile([P, O], U16, name="xr_codes", tag="read3", align_bytes=64)
+        nc.vector.tensor_copy(xr_codes[:], xr_table[:].indirect(l7[:]))
         out_banks = [psum.tile([P, O], F32, name="out_bank%d" % n) for n in range(2)]
         for n in range(2):
             nc.tensor.matmul_mx(out_banks[n][:], lhsT=ws_codes[:, n * P : (n + 1) * P].bitcast(FP8X4),

@@ -63,27 +63,22 @@ def tile_picked_tokens_codes_two_answered_reminder_plain_kernel(
             for r in range(4):
                 nc.sync.dma_start(plane[row + r : P : 32, :].bitcast(I32), rows[r])
 
-        def load_staged(src, cols, name, queue):
-            t = keep.tile([P, 2, cols // 4], I32, name=name, tag=name, align_bytes=64)
-            for h in range(2):
-                queue.dma_start(t[64 * h : 64 * h + 4, :, :],
-                                  src[0, 8 * h : 8 * h + 8, :].bitcast(I32).rearrange("(q r) n -> r q n", q=2))
+        def load_staged(src, cols, name):
+            t = keep.tile([4, 4, cols // 4], I32, name=name)
+            nc.sync.dma_start(t[:], src[0].bitcast(I32).rearrange("(q r) n -> r q n", r=4))
             return t
 
         def spread(plane, staged):
             for q in range(4):
-                nc.vector.tensor_copy(plane[32 * q : 32 * q + 4, :].bitcast(I32),
-                                      staged[64 * (q // 2) : 64 * (q // 2) + 4, q % 2, :])
+                nc.vector.tensor_copy(plane[32 * q : 32 * q + 4, :].bitcast(I32), staged[:, q, :])
 
-        w2_staged = load_staged(w2_scales, R, "w2_staged", nc.gpsimd)
-        xo_staged = load_staged(xo_scales, M, "xo_staged", nc.gpsimd)
         xt_plane = cleared_plane(T, "xt_plane", "xt_plane")
         w2_plane = cleared_plane(R, "w2_plane", "w2_plane")
         xo_plane = cleared_plane(M, "xo_plane", "xo_plane")
         boards = []
         for t in range(PACK):
             board = keep.tile([P, C], F32, name="board%d" % t)
-            nc.gpsimd.memset(board[:], 0.0)
+            nc.vector.memset(board[:], 0.0)
             boards.append(board)
         xr_plane = cleared_plane(V, "xr_plane", "xr_plane")
         wb_plane = cleared_plane(N, "wb_plane", "wb_plane")
@@ -95,9 +90,11 @@ def tile_picked_tokens_codes_two_answered_reminder_plain_kernel(
         l2 = load_list(offs2, "l2")
         ha_t = load_column(ha, "ha_t")
         l3 = load_list(offs3, "l3")
-        l1 = load_list(offs, "l1")
+        xo_staged = load_staged(xo_scales, M, "xo_staged")
+        w2_staged = load_staged(w2_scales, R, "w2_staged")
         nc.sync.dma_start(tables[1][:], ua_rows[:, 1, :])
         nc.sync.dma_start(tables[2][:], ua_rows[:, 2, :])
+        l1 = load_list(offs, "l1")
         load_plane(xt_plane, xt_scales, XT_ROW)
         nc.sync.dma_start(tables[3][:], ua_rows[:, 3, :])
         xo_table = load_words4(xo_words, M, "xo_table")
@@ -119,13 +116,13 @@ def tile_picked_tokens_codes_two_answered_reminder_plain_kernel(
         wc_planes = keep.tile([P, PACK, R], BF16, name="wc_planes")
         for t in range(PACK):
             nc.scalar.activation(wc_planes[:, t, :], tables[t][:].indirect(l2[:]), COPY, scale=ha_t[:, t : t + 1])
+        spread(xo_plane, xo_staged)
+        xo_sc = keep.tile([P, J], U8, name="xo_sc", align_bytes=64)
+        nc.vector.tensor_copy(xo_sc[:], xo_plane[:].indirect(l3[:]))
         spread(w2_plane, w2_staged)
         w2_sc = keep.tile([P, R], U8, name="w2_sc", align_bytes=64)
         nc.vector.tensor_copy(w2_sc[:].rearrange("p (u m) -> p u m", u=PACK),
                               w2_plane[:].rearrange("p (m u) -> p u m", u=PACK))
-        spread(xo_plane, xo_staged)
-        xo_sc = keep.tile([P, J], U8, name="xo_sc", align_bytes=64)
-        nc.vector.tensor_copy(xo_sc[:], xo_plane[:].indirect(l3[:]))
         xt_sc = keep.tile([P, J], U8, name="xt_sc", align_bytes=64)
         nc.vector.tensor_copy(xt_sc[:], xt_plane[:].indirect(l1[:]))
         xo_codes = keep.tile([P, J], U16, name="xo_codes", align_bytes=64)

@@ -18,8 +18,14 @@ MAX = mybir.AluOpType.max
 
 P = 128
 PACK = 4
+QUADS = 4
+QUAD = 32
+ROWS = 4
 LANES = 16
 XT_ROW = 4
+HJ = J // 2
+HO = O // 2
+RING = 3
 
 
 def tile_picked_tokens_codes_two_answered_reminder_plain_kernel(
@@ -34,61 +40,61 @@ def tile_picked_tokens_codes_two_answered_reminder_plain_kernel(
         psum = ctx.enter_context(tc.psum_pool(name="psum", bufs=1))
 
         def load_list(src, name):
-            t = lists.tile(list(src.shape), U16, name=name)
-            nc.sync.dma_start(t[:], src)
-            return t
+            tile = lists.tile(list(src.shape), U16, name=name)
+            nc.sync.dma_start(tile[:], src)
+            return tile
 
-        def load_column(src, name):
-            t = keep.tile([P, PACK], F32, name=name)
-            nc.sync.dma_start(t[:], src.rearrange("(p t) o -> p (t o)", t=PACK))
-            return t
+        def load_factors(src, name):
+            tile = keep.tile([P, PACK], F32, name=name)
+            nc.sync.dma_start(tile[:], src.rearrange("(p t) o -> p (t o)", t=PACK))
+            return tile
 
         def load_words8(src, cols, name):
-            t = keep.tile([P, cols], U32, name=name, tag=name, align_bytes=64)
-            nc.sync.dma_start(t[:].bitcast(I32), src[0].rearrange("p n t -> p (n t)").bitcast(I32))
-            return t
+            tile = keep.tile([P, cols], U32, name=name, tag=name, align_bytes=64)
+            nc.sync.dma_start(tile[:].bitcast(I32), src[0].rearrange("p n t -> p (n t)").bitcast(I32))
+            return tile
 
         def load_words4(src, cols, name):
-            t = keep.tile([P, cols], U16, name=name, align_bytes=64)
-            nc.sync.dma_start(t[:].bitcast(I32), src[0].bitcast(I32))
-            return t
+            tile = keep.tile([P, cols], U16, name=name, align_bytes=64)
+            nc.sync.dma_start(tile[:].bitcast(I32), src[0].bitcast(I32))
+            return tile
 
-        def cleared_plane(cols, name, tag):
-            t = keep.tile([P, cols], U8, name=name, tag=tag, align_bytes=64)
-            nc.vector.memset(t[:].bitcast(I32), 0)
-            return t
+        def cleared_plane(cols, name):
+            tile = keep.tile([P, cols], U8, name=name, align_bytes=64)
+            nc.vector.memset(tile[:].bitcast(I32), 0)
+            return tile
 
-        def load_plane(plane, src, row):
-            rows = src[0].bitcast(I32).rearrange("(q r) n -> r q n", r=4)
-            for r in range(4):
-                nc.sync.dma_start(plane[row + r : P : 32, :].bitcast(I32), rows[r])
+        def load_plane(plane, src, first_row):
+            rows = src[0].bitcast(I32).rearrange("(q i) n -> i q n", i=ROWS)
+            for i in range(ROWS):
+                nc.sync.dma_start(plane[first_row + i : P : QUAD, :].bitcast(I32), rows[i])
 
         def load_staged(src, cols, name):
-            t = keep.tile([4, 4, cols // 4], I32, name=name)
-            nc.sync.dma_start(t[:], src[0].bitcast(I32).rearrange("(q r) n -> r q n", r=4))
-            return t
+            tile = keep.tile([ROWS, QUADS, cols // 4], I32, name=name)
+            nc.sync.dma_start(tile[:], src[0].bitcast(I32).rearrange("(q i) n -> i q n", i=ROWS))
+            return tile
 
         def spread(plane, staged):
-            for q in range(4):
-                nc.vector.tensor_copy(plane[32 * q : 32 * q + 4, :].bitcast(I32), staged[:, q, :])
+            for q in range(QUADS):
+                nc.vector.tensor_copy(plane[QUAD * q : QUAD * q + ROWS, :].bitcast(I32), staged[:, q, :])
 
-        xt_plane = cleared_plane(T, "xt_plane", "xt_plane")
-        w2_plane = cleared_plane(R, "w2_plane", "w2_plane")
-        xo_plane = cleared_plane(M, "xo_plane", "xo_plane")
+        xt_plane = cleared_plane(T, "xt_plane")
+        w2_plane = cleared_plane(R, "w2_plane")
+        xo_plane = cleared_plane(M, "xo_plane")
         boards = []
-        for t in range(PACK):
-            board = keep.tile([P, C], F32, name="board%d" % t)
+        for u in range(PACK):
+            board = keep.tile([P, C], F32, name="board%d" % u, tag="board%d" % u, align_bytes=64)
             nc.vector.memset(board[:], 0.0)
             boards.append(board)
-        xr_plane = cleared_plane(V, "xr_plane", "xr_plane")
-        wb_plane = cleared_plane(N, "wb_plane", "wb_plane")
-        ws_plane = cleared_plane(N, "ws_plane", "ws_plane")
+        xr_plane = cleared_plane(V, "xr_plane")
+        wb_plane = cleared_plane(N, "wb_plane")
+        ws_plane = cleared_plane(N, "ws_plane")
 
         ua_rows = ua.rearrange("(p t) f -> p t f", t=PACK)
         tables = [keep.tile([P, F], F32, name="table%d" % t) for t in range(PACK)]
         nc.sync.dma_start(tables[0][:], ua_rows[:, 0, :])
         l2 = load_list(offs2, "l2")
-        ha_t = load_column(ha, "ha_t")
+        ha_t = load_factors(ha, "ha_t")
         l3 = load_list(offs3, "l3")
         xo_staged = load_staged(xo_scales, M, "xo_staged")
         w2_staged = load_staged(w2_scales, R, "w2_staged")
@@ -102,9 +108,9 @@ def tile_picked_tokens_codes_two_answered_reminder_plain_kernel(
         l4 = load_list(offs4, "l4")
         w2_raw = load_words8(w2_words, R, "w2_raw")
         l5 = load_list(offs5, "l5")
-        sa_t = load_column(sa, "sa_t")
+        sa_t = load_factors(sa, "sa_t")
         l6 = load_list(offs6, "l6")
-        sb_t = load_column(sb, "sb_t")
+        sb_t = load_factors(sb, "sb_t")
         l7 = load_list(offs7, "l7")
         xr_table = load_words4(xr_words, V, "xr_table")
         load_plane(xr_plane, xr_scales, 0)
@@ -113,9 +119,10 @@ def tile_picked_tokens_codes_two_answered_reminder_plain_kernel(
         wb_codes = load_words8(wb_words, N, "wb_codes")
         load_plane(wb_plane, wb_scales, 0)
 
-        wc_planes = keep.tile([P, PACK, R], BF16, name="wc_planes")
+        wc_slots = keep.tile([P, PACK, R], BF16, name="wc_slots")
         for t in range(PACK):
-            nc.scalar.activation(wc_planes[:, t, :], tables[t][:].indirect(l2[:]), COPY, scale=ha_t[:, t : t + 1])
+            nc.scalar.activation(wc_slots[:, t, :], tables[t][:].indirect(l2[:]), COPY, scale=ha_t[:, t : t + 1])
+
         spread(xo_plane, xo_staged)
         xo_sc = keep.tile([P, J], U8, name="xo_sc", align_bytes=64)
         nc.vector.tensor_copy(xo_sc[:], xo_plane[:].indirect(l3[:]))
@@ -128,40 +135,44 @@ def tile_picked_tokens_codes_two_answered_reminder_plain_kernel(
         xo_codes = keep.tile([P, J], U16, name="xo_codes", align_bytes=64)
         nc.vector.tensor_copy(xo_codes[:], xo_table[:].indirect(l3[:]))
 
-        wc_dealt = wc_planes[:].rearrange("p t (m u) -> p u m t", u=PACK)
-        wc_in = [keep.tile([P, w, P, PACK], BF16, name="wc_in%d" % w, align_bytes=64) for w in (1, 3)]
-        wc_sc = [keep.tile([P, w * P], U8, name="wc_sc%d" % w, align_bytes=64) for w in (1, 3)]
+        wc_dealt = wc_slots[:].rearrange("p t (m u) -> p u m t", u=PACK)
+        groups = (1, PACK - 1)
+        wc_in = [keep.tile([P, w, P, PACK], BF16, name="wc_in%d" % w, align_bytes=64) for w in groups]
+        wc_sc = [keep.tile([P, w * P], U8, name="wc_sc%d" % w, align_bytes=64) for w in groups]
         wc_codes = [keep.tile([P, P], U32, name="wc_codes_first", align_bytes=64)]
         nc.vector.tensor_copy(wc_in[0][:, 0], wc_dealt[:, 0])
         for u in range(1, PACK):
             nc.scalar.copy(wc_in[1][:, u - 1], wc_dealt[:, u])
         nc.vector.quantize_mx(wc_codes[0][:].bitcast(FP8X4), wc_sc[0][:], wc_in[0][:].rearrange("p u m t -> p (u m t)"))
 
-        xt_codes = [keep.tile([P, J // 2], U32, name="xt_codes%d" % h, align_bytes=64) for h in range(2)]
-        HJ = J // 2
+        xt_codes = [keep.tile([P, HJ], U32, name="xt_codes%d" % h, align_bytes=64) for h in range(2)]
         for h in range(2):
             nc.vector.tensor_copy(xt_codes[h][:], xt_table[:].indirect(l1[:, h * HJ // LANES : (h + 1) * HJ // LANES]))
-        wc_codes.append(keep.tile([P, 3 * P], U32, name="wc_codes_rest", tag="xt_table", align_bytes=64))
+        wc_codes.append(keep.tile([P, groups[1] * P], U32, name="wc_codes_rest", tag="xt_table", align_bytes=64))
         nc.vector.quantize_mx(wc_codes[1][:].bitcast(FP8X4), wc_sc[1][:], wc_in[1][:].rearrange("p u m t -> p (u m t)"))
 
-        def first_product(bank, u, h):
-            i, c = min(u, 1), max(u - 1, 0) * P
-            nc.tensor.matmul_mx(bank, lhsT=wc_codes[i][:, c : c + P].bitcast(FP8X4), lhsT_scale=wc_sc[i][:, c : c + P],
-                                rhs=xt_codes[h][:].bitcast(FP8X4), rhs_scale=xt_sc[XT_ROW:P, h * HJ : (h + 1) * HJ],
-                                start=True, stop=True)
+        def a_bank():
+            return psum.tile([P, J], F32, name="a_bank", tag="a_bank", bufs=RING)
 
-        a_sb = [keep.tile([P, J], F32, name="a_sb%d" % u, tag="a_sb%d" % u, align_bytes=64) for u in range(PACK)]
+        def matmul_a(target, u, h):
+            group, col = min(u, 1), max(u - 1, 0) * P
+            nc.tensor.matmul_mx(target, lhsT=wc_codes[group][:, col : col + P].bitcast(FP8X4),
+                                lhsT_scale=wc_sc[group][:, col : col + P], rhs=xt_codes[h][:].bitcast(FP8X4),
+                                rhs_scale=xt_sc[XT_ROW:P, h * HJ : (h + 1) * HJ], start=True, stop=True)
+
+        a_sb = [keep.tile([P, J], F32, name="a_sb%d" % u, align_bytes=64) for u in range(PACK)]
         for h in range(2):
-            bank = psum.tile([P, J], F32, name="a_bank", tag="a_bank", bufs=3)
-            first_product(bank[:, 0:HJ], 0, h)
+            bank = a_bank()
+            matmul_a(bank[:, 0:HJ], 0, h)
             nc.scalar.copy(a_sb[0][:, h * HJ : (h + 1) * HJ], bank[:, 0:HJ])
-        nc.vector.tensor_copy(boards[0][:].indirect(l4[:, 0 : HJ // LANES]), a_sb[0][:, 0:HJ])
-        nc.vector.tensor_copy(boards[0][:].indirect(l4[:, HJ // LANES : J // LANES]), a_sb[0][:, HJ:J])
+        for h in range(2):
+            nc.vector.tensor_copy(boards[0][:].indirect(l4[:, h * HJ // LANES : (h + 1) * HJ // LANES]),
+                                  a_sb[0][:, h * HJ : (h + 1) * HJ])
 
         def product_a(u):
-            bank = psum.tile([P, J], F32, name="a_bank", tag="a_bank", bufs=3)
+            bank = a_bank()
             for h in range(2):
-                first_product(bank[:, h * HJ : (h + 1) * HJ], u, h)
+                matmul_a(bank[:, h * HJ : (h + 1) * HJ], u, h)
             nc.scalar.copy(a_sb[u][:], bank[:])
 
         def scatter(u):
@@ -173,74 +184,72 @@ def tile_picked_tokens_codes_two_answered_reminder_plain_kernel(
         scatter(1)
 
         b_banks = {}
+        fetched = [keep.tile([P, J], F32, name="fetched%d" % u, align_bytes=64) for u in range(PACK)]
+        g1 = {}
+        hid_slots = keep.tile([P, PACK, O], BF16, name="hid_slots")
 
         def product_b(u):
-            b_banks[u] = psum.tile([P, J], F32, name="b_bank", tag="b_bank", bufs=3)
+            b_banks[u] = psum.tile([P, J], F32, name="b_bank", tag="b_bank", bufs=RING)
             nc.tensor.matmul_mx(b_banks[u][:], lhsT=w2_codes[:, u * P : (u + 1) * P].bitcast(FP8X4),
                                 lhsT_scale=w2_sc[:, u * P : (u + 1) * P], rhs=xo_codes[:].bitcast(FP4X4),
                                 rhs_scale=xo_sc[:], start=True, stop=True)
 
-        read = [keep.tile([P, J], F32, name="read%d" % u, tag="read%d" % u, align_bytes=64) for u in range(PACK)]
-        g1 = {}
-        hid_planes = keep.tile([P, PACK, O], BF16, name="hid_planes")
+        def read_board(u):
+            nc.scalar.activation(fetched[u][:], boards[u][:].indirect(l5[:]), COPY, scale=sa_t[:, u : u + 1])
 
-        def read_board(u, lo, hi):
-            nc.scalar.activation(read[u][:, lo:hi], boards[u][:].indirect(l5[:, lo // LANES : hi // LANES]), COPY,
-                                 scale=sa_t[:, u : u + 1])
-
-        def larger(u, lo, hi):
-            if lo == 0:
-                g1[u] = keep.tile([P, J], F32, name="g1_%d" % u, tag="a_sb%d" % ((u + 1) % PACK), align_bytes=64)
-            nc.vector.tensor_tensor(g1[u][:, lo:hi], read[u][:, lo:hi], b_banks[u][:, lo:hi], MAX)
+        def larger(u):
+            g1[u] = keep.tile([P, J], F32, name="g1_%d" % u)
+            nc.vector.tensor_tensor(g1[u][:], fetched[u][:], b_banks[u][:], MAX)
 
         def answers(u, lo, hi):
-            nc.scalar.activation(hid_planes[:, u, lo:hi], g1[u][:].indirect(l6[:, lo // LANES : hi // LANES]), COPY,
+            nc.scalar.activation(hid_slots[:, u, lo:hi], g1[u][:].indirect(l6[:, lo // LANES : hi // LANES]), COPY,
                                  scale=sb_t[:, u : u + 1])
 
         product_b(0)
-        read_board(0, 0, J)
-        product_a(2)
-        product_b(1)
-        larger(0, 0, J)
-        scatter(2)
-        read_board(1, 0, J)
-        product_a(3)
-        product_b(2)
-        answers(0, 0, O)
-        larger(1, 0, J)
-        scatter(3)
+        for u in range(2):
+            read_board(u)
+            product_a(u + 2)
+            product_b(u + 1)
+            if u > 0:
+                answers(u - 1, 0, O)
+            larger(u)
+            scatter(u + 2)
         product_b(3)
-        read_board(2, 0, J)
+        read_board(2)
         answers(1, 0, O)
-        larger(2, 0, J)
-        xr_sc = keep.tile([P, O], U8, name="xr_sc", tag="read2", align_bytes=64)
+        larger(2)
+        xr_sc = keep.tile([P, O], U8, name="xr_sc", tag="board2", align_bytes=64)
         nc.vector.tensor_copy(xr_sc[:], xr_plane[:].indirect(l7[:]))
-        read_board(3, 0, J)
+        read_board(3)
         answers(2, 0, O)
-        larger(3, 0, J)
-        xr_codes = keep.tile([P, O], U16, name="xr_codes", tag="read3", align_bytes=64)
+        larger(3)
+        xr_codes = keep.tile([P, O], U16, name="xr_codes", tag="board3", align_bytes=64)
         nc.vector.tensor_copy(xr_codes[:], xr_table[:].indirect(l7[:]))
-        out_banks = [psum.tile([P, O], F32, name="out_bank%d" % n) for n in range(2)]
-        for n in range(2):
-            nc.tensor.matmul_mx(out_banks[n][:], lhsT=ws_codes[:, n * P : (n + 1) * P].bitcast(FP8X4),
-                                lhsT_scale=ws_plane[:, n * P : (n + 1) * P], rhs=xr_codes[:].bitcast(FP4X4),
-                                rhs_scale=xr_sc[:], start=True, stop=False)
-        HO = O // 2
+
+        out_banks = {}
+        for h in range(2):
+            for n in range(2):
+                out_banks[h, n] = a_bank() if h == 0 else psum.tile([P, J], F32, name="out_bank%d" % n)
+                nc.tensor.matmul_mx(out_banks[h, n][:, 0:HO], lhsT=ws_codes[:, n * P : (n + 1) * P].bitcast(FP8X4),
+                                    lhsT_scale=ws_plane[:, n * P : (n + 1) * P],
+                                    rhs=xr_codes[:, h * HO : (h + 1) * HO].bitcast(FP4X4),
+                                    rhs_scale=xr_sc[:, h * HO : (h + 1) * HO], start=True, stop=False)
         hid_in = [keep.tile([P, HO, PACK], BF16, name="hid_in%d" % h, align_bytes=64) for h in range(2)]
         hid_codes = [keep.tile([P, HO], U32, name="hid_codes%d" % h, align_bytes=64) for h in range(2)]
         hid_sc = [keep.tile([P, HO], U8, name="hid_sc%d" % h, align_bytes=64) for h in range(2)]
         for h in range(2):
             answers(3, h * HO, (h + 1) * HO)
         for h in range(2):
-            nc.vector.tensor_copy(hid_in[h][:], hid_planes[:, :, h * HO : (h + 1) * HO].rearrange("p t o -> p o t"))
+            nc.vector.tensor_copy(hid_in[h][:], hid_slots[:, :, h * HO : (h + 1) * HO].rearrange("p t o -> p o t"))
         for h in range(2):
             nc.vector.quantize_mx(hid_codes[h][:].bitcast(FP8X4), hid_sc[h][:], hid_in[h][:].rearrange("p o t -> p (o t)"))
             for n in range(2):
-                nc.tensor.matmul_mx(out_banks[n][:, h * HO : (h + 1) * HO], lhsT=wb_codes[:, n * P : (n + 1) * P].bitcast(FP8X4),
+                nc.tensor.matmul_mx(out_banks[h, n][:, 0:HO], lhsT=wb_codes[:, n * P : (n + 1) * P].bitcast(FP8X4),
                                     lhsT_scale=wb_plane[:, n * P : (n + 1) * P], rhs=hid_codes[h][:].bitcast(FP8X4),
-                                    rhs_scale=hid_sc[h][:], start=False, stop=(h == 1))
-        result = [keep.tile([P, O], F32, name="result%d" % n) for n in range(2)]
-        nc.scalar.copy(result[0][:], out_banks[0][:])
-        nc.scalar.dma_start(out[0:P, :], result[0][:])
-        nc.vector.tensor_copy(result[1][:], out_banks[1][:])
-        nc.sync.dma_start(out[P : 2 * P, :], result[1][:])
+                                    rhs_scale=hid_sc[h][:], start=False, stop=True)
+        for h in range(2):
+            result = [keep.tile([P, HO], F32, name="result%d%d" % (h, n)) for n in range(2)]
+            nc.scalar.copy(result[0][:], out_banks[h, 0][:, 0:HO])
+            nc.scalar.dma_start(out[0:P, h * HO : (h + 1) * HO], result[0][:])
+            nc.vector.tensor_copy(result[1][:], out_banks[h, 1][:, 0:HO])
+            nc.sync.dma_start(out[P : 2 * P, h * HO : (h + 1) * HO], result[1][:])

@@ -1,6 +1,7 @@
 from contextlib import ExitStack
 
 import concourse.mybir as mybir
+from concourse.masks import make_identity
 
 K, J, R, T, F, Z, M, O, C, N, S, V = 512, 512, 512, 2048, 2048, 512, 1024, 256, 1024, 256, 512, 1024
 FLOPS = 2 * K * R * J + 2 * Z * R * J + 2 * R * N * O + 2 * S * N * O
@@ -26,6 +27,7 @@ XT_ROW = 4
 HJ = J // 2
 HO = O // 2
 RING = 3
+SPARE = 2
 
 
 def tile_picked_tokens_codes_two_answered_reminder_plain_kernel(
@@ -78,14 +80,16 @@ def tile_picked_tokens_codes_two_answered_reminder_plain_kernel(
             for q in range(QUADS):
                 nc.vector.tensor_copy(plane[QUAD * q : QUAD * q + ROWS, :].bitcast(I32), staged[:, q, :])
 
+        identity = keep.tile([P, P], F32, name="identity")
+        make_identity(nc, identity[:])
         xt_plane = cleared_plane(T, "xt_plane")
-        w2_plane = cleared_plane(R, "w2_plane")
         xo_plane = cleared_plane(M, "xo_plane")
         boards = []
         for u in range(PACK):
             board = keep.tile([P, C], F32, name="board%d" % u, tag="board%d" % u, align_bytes=64)
             nc.vector.memset(board[:], 0.0)
             boards.append(board)
+        w2_plane = cleared_plane(R, "w2_plane")
         xr_plane = cleared_plane(V, "xr_plane")
         wb_plane = cleared_plane(N, "wb_plane")
         ws_plane = cleared_plane(N, "ws_plane")
@@ -97,7 +101,6 @@ def tile_picked_tokens_codes_two_answered_reminder_plain_kernel(
         ha_t = load_factors(ha, "ha_t")
         l3 = load_list(offs3, "l3")
         xo_staged = load_staged(xo_scales, M, "xo_staged")
-        w2_staged = load_staged(w2_scales, R, "w2_staged")
         nc.sync.dma_start(tables[1][:], ua_rows[:, 1, :])
         nc.sync.dma_start(tables[2][:], ua_rows[:, 2, :])
         l1 = load_list(offs, "l1")
@@ -106,7 +109,8 @@ def tile_picked_tokens_codes_two_answered_reminder_plain_kernel(
         xo_table = load_words4(xo_words, M, "xo_table")
         xt_table = load_words8(xt_words, T, "xt_table")
         l4 = load_list(offs4, "l4")
-        w2_raw = load_words8(w2_words, R, "w2_raw")
+        w2_codes = load_words8(w2_words, R, "w2_codes")
+        load_plane(w2_plane, w2_scales, 0)
         l5 = load_list(offs5, "l5")
         sa_t = load_factors(sa, "sa_t")
         l6 = load_list(offs6, "l6")
@@ -126,10 +130,6 @@ def tile_picked_tokens_codes_two_answered_reminder_plain_kernel(
         spread(xo_plane, xo_staged)
         xo_sc = keep.tile([P, J], U8, name="xo_sc", align_bytes=64)
         nc.vector.tensor_copy(xo_sc[:], xo_plane[:].indirect(l3[:]))
-        spread(w2_plane, w2_staged)
-        w2_sc = keep.tile([P, R], U8, name="w2_sc", align_bytes=64)
-        nc.vector.tensor_copy(w2_sc[:].rearrange("p (u m) -> p u m", u=PACK),
-                              w2_plane[:].rearrange("p (m u) -> p u m", u=PACK))
         xt_sc = keep.tile([P, J], U8, name="xt_sc", align_bytes=64)
         nc.vector.tensor_copy(xt_sc[:], xt_plane[:].indirect(l1[:]))
         xo_codes = keep.tile([P, J], U16, name="xo_codes", align_bytes=64)
@@ -153,6 +153,9 @@ def tile_picked_tokens_codes_two_answered_reminder_plain_kernel(
 
         def a_bank():
             return psum.tile([P, J], F32, name="a_bank", tag="a_bank", bufs=RING)
+
+        def spare_bank():
+            return psum.tile([P, R], F32, name="spare_bank", tag="spare_bank", bufs=SPARE)
 
         def matmul_a(target, u, h):
             group, col = min(u, 1), max(u - 1, 0) * P
@@ -179,8 +182,13 @@ def tile_picked_tokens_codes_two_answered_reminder_plain_kernel(
             nc.vector.tensor_copy(boards[u][:].indirect(l4[:]), a_sb[u][:])
 
         product_a(1)
-        w2_codes = keep.tile([P, R], U32, name="w2_codes", align_bytes=64)
-        nc.scalar.copy(w2_codes[:].rearrange("p (u m) -> p m u", u=PACK), w2_raw[:].rearrange("p (m u) -> p m u", u=PACK))
+        turned = keep.tile([P, J // P, R], F32, name="turned")
+        for i in range(J // P):
+            bank = spare_bank()
+            nc.tensor.matmul_mx(bank[:], lhsT=xo_codes[:, i * P : (i + 1) * P].bitcast(FP4X4),
+                                lhsT_scale=xo_sc[:, i * P : (i + 1) * P], rhs=w2_codes[:].bitcast(FP8X4),
+                                rhs_scale=w2_plane[:], start=True, stop=True)
+            nc.scalar.copy(turned[:, i, :], bank[:])
         scatter(1)
 
         b_banks = {}
@@ -188,11 +196,10 @@ def tile_picked_tokens_codes_two_answered_reminder_plain_kernel(
         g1 = {}
         hid_slots = keep.tile([P, PACK, O], BF16, name="hid_slots")
 
-        def product_b(u):
+        def turn_b(u):
             b_banks[u] = psum.tile([P, J], F32, name="b_bank", tag="b_bank", bufs=RING)
-            nc.tensor.matmul_mx(b_banks[u][:], lhsT=w2_codes[:, u * P : (u + 1) * P].bitcast(FP8X4),
-                                lhsT_scale=w2_sc[:, u * P : (u + 1) * P], rhs=xo_codes[:].bitcast(FP4X4),
-                                rhs_scale=xo_sc[:], start=True, stop=True)
+            for i in range(J // P):
+                nc.tensor.transpose(b_banks[u][:, i * P : (i + 1) * P], turned[:, i, u:R:PACK], identity[:])
 
         def read_board(u):
             nc.scalar.activation(fetched[u][:], boards[u][:].indirect(l5[:]), COPY, scale=sa_t[:, u : u + 1])
@@ -205,16 +212,16 @@ def tile_picked_tokens_codes_two_answered_reminder_plain_kernel(
             nc.scalar.activation(hid_slots[:, u, lo:hi], g1[u][:].indirect(l6[:, lo // LANES : hi // LANES]), COPY,
                                  scale=sb_t[:, u : u + 1])
 
-        product_b(0)
+        turn_b(0)
         for u in range(2):
             read_board(u)
             product_a(u + 2)
-            product_b(u + 1)
+            turn_b(u + 1)
             if u > 0:
                 answers(u - 1, 0, O)
             larger(u)
             scatter(u + 2)
-        product_b(3)
+        turn_b(3)
         read_board(2)
         answers(1, 0, O)
         larger(2)
@@ -229,7 +236,7 @@ def tile_picked_tokens_codes_two_answered_reminder_plain_kernel(
         out_banks = {}
         for h in range(2):
             for n in range(2):
-                out_banks[h, n] = a_bank() if h == 0 else psum.tile([P, J], F32, name="out_bank%d" % n)
+                out_banks[h, n] = a_bank() if h == 0 else spare_bank()
                 nc.tensor.matmul_mx(out_banks[h, n][:, 0:HO], lhsT=ws_codes[:, n * P : (n + 1) * P].bitcast(FP8X4),
                                     lhsT_scale=ws_plane[:, n * P : (n + 1) * P],
                                     rhs=xr_codes[:, h * HO : (h + 1) * HO].bitcast(FP4X4),

from contextlib import ExitStack

import concourse.mybir as mybir
from concourse.masks import make_identity

K, J, R, T, F, Z, M, O, C, N, S, V = 512, 512, 512, 2048, 2048, 512, 1024, 256, 1024, 256, 512, 1024
FLOPS = 2 * K * R * J + 2 * Z * R * J + 2 * R * N * O + 2 * S * N * O

F32 = mybir.dt.float32
BF16 = mybir.dt.bfloat16
I32 = mybir.dt.int32
U32 = mybir.dt.uint32
U16 = mybir.dt.uint16
U8 = mybir.dt.uint8
FP8X4 = mybir.dt.float8_e4m3fn_x4
FP4X4 = mybir.dt.float4_e2m1fn_x4
COPY = mybir.ActivationFunctionType.Copy
MAX = mybir.AluOpType.max

P = 128
PACK = 4
QUADS = 4
QUAD = 32
ROWS = 4
LANES = 16
XT_ROW = 4
HJ = J // 2
HO = O // 2
RING = 3
SPARE = 2


def tile_picked_tokens_codes_two_answered_reminder_plain_kernel(
    tc, xt_words, xt_scales, ua, ha, xo_words, xo_scales, w2_words, w2_scales, sa, sb,
    wb_words, wb_scales, xr_words, xr_scales, ws_words, ws_scales,
    offs, offs2, offs3, offs4, offs5, offs6, offs7, out,
):
    nc = tc.nc
    with ExitStack() as ctx:
        lists = ctx.enter_context(tc.tile_pool(name="lists", bufs=1))
        keep = ctx.enter_context(tc.tile_pool(name="keep", bufs=1))
        psum = ctx.enter_context(tc.psum_pool(name="psum", bufs=1))

        def load_list(src, name):
            tile = lists.tile(list(src.shape), U16, name=name)
            nc.sync.dma_start(tile[:], src)
            return tile

        def load_factors(src, name):
            tile = keep.tile([P, PACK], F32, name=name)
            nc.sync.dma_start(tile[:], src.rearrange("(p t) o -> p (t o)", t=PACK))
            return tile

        def load_words8(src, cols, name):
            tile = keep.tile([P, cols], U32, name=name, tag=name, align_bytes=64)
            nc.sync.dma_start(tile[:].bitcast(I32), src[0].rearrange("p n t -> p (n t)").bitcast(I32))
            return tile

        def load_words4(src, cols, name):
            tile = keep.tile([P, cols], U16, name=name, align_bytes=64)
            nc.sync.dma_start(tile[:].bitcast(I32), src[0].bitcast(I32))
            return tile

        def cleared_plane(cols, name):
            tile = keep.tile([P, cols], U8, name=name, align_bytes=64)
            nc.vector.memset(tile[:].bitcast(I32), 0)
            return tile

        def load_plane(plane, src, first_row):
            rows = src[0].bitcast(I32).rearrange("(q i) n -> i q n", i=ROWS)
            for i in range(ROWS):
                nc.sync.dma_start(plane[first_row + i : P : QUAD, :].bitcast(I32), rows[i])

        def load_staged(src, cols, name):
            tile = keep.tile([ROWS, QUADS, cols // 4], I32, name=name)
            nc.sync.dma_start(tile[:], src[0].bitcast(I32).rearrange("(q i) n -> i q n", i=ROWS))
            return tile

        def spread(plane, staged):
            for q in range(QUADS):
                nc.vector.tensor_copy(plane[QUAD * q : QUAD * q + ROWS, :].bitcast(I32), staged[:, q, :])

        identity = keep.tile([P, P], F32, name="identity")
        make_identity(nc, identity[:])
        xt_plane = cleared_plane(T, "xt_plane")
        xo_plane = cleared_plane(M, "xo_plane")
        boards = []
        for u in range(PACK):
            board = keep.tile([P, C], F32, name="board%d" % u, tag="board%d" % u, align_bytes=64)
            nc.vector.memset(board[:], 0.0)
            boards.append(board)
        w2_plane = cleared_plane(R, "w2_plane")
        xr_plane = cleared_plane(V, "xr_plane")
        wb_plane = cleared_plane(N, "wb_plane")
        ws_plane = cleared_plane(N, "ws_plane")

        ua_rows = ua.rearrange("(p t) f -> p t f", t=PACK)
        tables = [keep.tile([P, F], F32, name="table%d" % t) for t in range(PACK)]
        nc.sync.dma_start(tables[0][:], ua_rows[:, 0, :])
        l2 = load_list(offs2, "l2")
        ha_t = load_factors(ha, "ha_t")
        l3 = load_list(offs3, "l3")
        xo_staged = load_staged(xo_scales, M, "xo_staged")
        nc.sync.dma_start(tables[1][:], ua_rows[:, 1, :])
        nc.sync.dma_start(tables[2][:], ua_rows[:, 2, :])
        l1 = load_list(offs, "l1")
        load_plane(xt_plane, xt_scales, XT_ROW)
        nc.sync.dma_start(tables[3][:], ua_rows[:, 3, :])
        xo_table = load_words4(xo_words, M, "xo_table")
        xt_table = load_words8(xt_words, T, "xt_table")
        l4 = load_list(offs4, "l4")
        w2_codes = load_words8(w2_words, R, "w2_codes")
        load_plane(w2_plane, w2_scales, 0)
        l5 = load_list(offs5, "l5")
        sa_t = load_factors(sa, "sa_t")
        l6 = load_list(offs6, "l6")
        sb_t = load_factors(sb, "sb_t")
        l7 = load_list(offs7, "l7")
        xr_table = load_words4(xr_words, V, "xr_table")
        load_plane(xr_plane, xr_scales, 0)
        ws_codes = load_words8(ws_words, N, "ws_codes")
        load_plane(ws_plane, ws_scales, 0)
        wb_codes = load_words8(wb_words, N, "wb_codes")
        load_plane(wb_plane, wb_scales, 0)

        wc_slots = keep.tile([P, PACK, R], BF16, name="wc_slots")
        for t in range(PACK):
            nc.scalar.activation(wc_slots[:, t, :], tables[t][:].indirect(l2[:]), COPY, scale=ha_t[:, t : t + 1])

        spread(xo_plane, xo_staged)
        xo_sc = keep.tile([P, J], U8, name="xo_sc", align_bytes=64)
        nc.vector.tensor_copy(xo_sc[:], xo_plane[:].indirect(l3[:]))
        xt_sc = keep.tile([P, J], U8, name="xt_sc", align_bytes=64)
        nc.vector.tensor_copy(xt_sc[:], xt_plane[:].indirect(l1[:]))
        xo_codes = keep.tile([P, J], U16, name="xo_codes", align_bytes=64)
        nc.vector.tensor_copy(xo_codes[:], xo_table[:].indirect(l3[:]))

        wc_dealt = wc_slots[:].rearrange("p t (m u) -> p u m t", u=PACK)
        groups = (1, PACK - 1)
        wc_in = [keep.tile([P, w, P, PACK], BF16, name="wc_in%d" % w, align_bytes=64) for w in groups]
        wc_sc = [keep.tile([P, w * P], U8, name="wc_sc%d" % w, align_bytes=64) for w in groups]
        wc_codes = [keep.tile([P, P], U32, name="wc_codes_first", align_bytes=64)]
        nc.vector.tensor_copy(wc_in[0][:, 0], wc_dealt[:, 0])
        for u in range(1, PACK):
            nc.scalar.copy(wc_in[1][:, u - 1], wc_dealt[:, u])
        nc.vector.quantize_mx(wc_codes[0][:].bitcast(FP8X4), wc_sc[0][:], wc_in[0][:].rearrange("p u m t -> p (u m t)"))

        xt_codes = [keep.tile([P, HJ], U32, name="xt_codes%d" % h, align_bytes=64) for h in range(2)]
        for h in range(2):
            nc.vector.tensor_copy(xt_codes[h][:], xt_table[:].indirect(l1[:, h * HJ // LANES : (h + 1) * HJ // LANES]))
        wc_codes.append(keep.tile([P, groups[1] * P], U32, name="wc_codes_rest", tag="xt_table", align_bytes=64))
        nc.vector.quantize_mx(wc_codes[1][:].bitcast(FP8X4), wc_sc[1][:], wc_in[1][:].rearrange("p u m t -> p (u m t)"))

        def a_bank():
            return psum.tile([P, J], F32, name="a_bank", tag="a_bank", bufs=RING)

        def spare_bank():
            return psum.tile([P, R], F32, name="spare_bank", tag="spare_bank", bufs=SPARE)

        def matmul_a(target, u, h):
            group, col = min(u, 1), max(u - 1, 0) * P
            nc.tensor.matmul_mx(target, lhsT=wc_codes[group][:, col : col + P].bitcast(FP8X4),
                                lhsT_scale=wc_sc[group][:, col : col + P], rhs=xt_codes[h][:].bitcast(FP8X4),
                                rhs_scale=xt_sc[XT_ROW:P, h * HJ : (h + 1) * HJ], start=True, stop=True)

        a_sb = [keep.tile([P, J], F32, name="a_sb%d" % u, align_bytes=64) for u in range(PACK)]
        for h in range(2):
            bank = a_bank()
            matmul_a(bank[:, 0:HJ], 0, h)
            nc.scalar.copy(a_sb[0][:, h * HJ : (h + 1) * HJ], bank[:, 0:HJ])
        for h in range(2):
            nc.vector.tensor_copy(boards[0][:].indirect(l4[:, h * HJ // LANES : (h + 1) * HJ // LANES]),
                                  a_sb[0][:, h * HJ : (h + 1) * HJ])

        def product_a(u):
            bank = a_bank()
            for h in range(2):
                matmul_a(bank[:, h * HJ : (h + 1) * HJ], u, h)
            nc.scalar.copy(a_sb[u][:], bank[:])

        def scatter(u):
            nc.vector.tensor_copy(boards[u][:].indirect(l4[:]), a_sb[u][:])

        product_a(1)
        turned = keep.tile([P, J // P, R], F32, name="turned")
        for i in range(J // P):
            bank = spare_bank()
            nc.tensor.matmul_mx(bank[:], lhsT=xo_codes[:, i * P : (i + 1) * P].bitcast(FP4X4),
                                lhsT_scale=xo_sc[:, i * P : (i + 1) * P], rhs=w2_codes[:].bitcast(FP8X4),
                                rhs_scale=w2_plane[:], start=True, stop=True)
            nc.scalar.copy(turned[:, i, :], bank[:])
        scatter(1)

        b_banks = {}
        fetched = [keep.tile([P, J], F32, name="fetched%d" % u, align_bytes=64) for u in range(PACK)]
        g1 = {}
        hid_slots = keep.tile([P, PACK, O], BF16, name="hid_slots")

        def turn_b(u):
            b_banks[u] = psum.tile([P, J], F32, name="b_bank", tag="b_bank", bufs=RING)
            for i in range(J // P):
                nc.tensor.transpose(b_banks[u][:, i * P : (i + 1) * P], turned[:, i, u:R:PACK], identity[:])

        def read_board(u):
            nc.scalar.activation(fetched[u][:], boards[u][:].indirect(l5[:]), COPY, scale=sa_t[:, u : u + 1])

        def larger(u):
            g1[u] = keep.tile([P, J], F32, name="g1_%d" % u)
            nc.vector.tensor_tensor(g1[u][:], fetched[u][:], b_banks[u][:], MAX)

        def answers(u, lo, hi):
            nc.scalar.activation(hid_slots[:, u, lo:hi], g1[u][:].indirect(l6[:, lo // LANES : hi // LANES]), COPY,
                                 scale=sb_t[:, u : u + 1])

        turn_b(0)
        for u in range(2):
            read_board(u)
            product_a(u + 2)
            turn_b(u + 1)
            if u > 0:
                answers(u - 1, 0, O)
            larger(u)
            scatter(u + 2)
        turn_b(3)
        read_board(2)
        answers(1, 0, O)
        larger(2)
        xr_sc = keep.tile([P, O], U8, name="xr_sc", tag="board2", align_bytes=64)
        nc.vector.tensor_copy(xr_sc[:], xr_plane[:].indirect(l7[:]))
        read_board(3)
        answers(2, 0, O)
        larger(3)
        xr_codes = keep.tile([P, O], U16, name="xr_codes", tag="board3", align_bytes=64)
        nc.vector.tensor_copy(xr_codes[:], xr_table[:].indirect(l7[:]))

        out_banks = {}
        for h in range(2):
            for n in range(2):
                out_banks[h, n] = a_bank() if h == 0 else spare_bank()
                nc.tensor.matmul_mx(out_banks[h, n][:, 0:HO], lhsT=ws_codes[:, n * P : (n + 1) * P].bitcast(FP8X4),
                                    lhsT_scale=ws_plane[:, n * P : (n + 1) * P],
                                    rhs=xr_codes[:, h * HO : (h + 1) * HO].bitcast(FP4X4),
                                    rhs_scale=xr_sc[:, h * HO : (h + 1) * HO], start=True, stop=False)
        hid_in = [keep.tile([P, HO, PACK], BF16, name="hid_in%d" % h, align_bytes=64) for h in range(2)]
        hid_codes = [keep.tile([P, HO], U32, name="hid_codes%d" % h, align_bytes=64) for h in range(2)]
        hid_sc = [keep.tile([P, HO], U8, name="hid_sc%d" % h, align_bytes=64) for h in range(2)]
        for h in range(2):
            answers(3, h * HO, (h + 1) * HO)
        for h in range(2):
            nc.vector.tensor_copy(hid_in[h][:], hid_slots[:, :, h * HO : (h + 1) * HO].rearrange("p t o -> p o t"))
        for h in range(2):
            nc.vector.quantize_mx(hid_codes[h][:].bitcast(FP8X4), hid_sc[h][:], hid_in[h][:].rearrange("p o t -> p (o t)"))
            for n in range(2):
                nc.tensor.matmul_mx(out_banks[h, n][:, 0:HO], lhsT=wb_codes[:, n * P : (n + 1) * P].bitcast(FP8X4),
                                    lhsT_scale=wb_plane[:, n * P : (n + 1) * P], rhs=hid_codes[h][:].bitcast(FP8X4),
                                    rhs_scale=hid_sc[h][:], start=False, stop=True)
        for h in range(2):
            result = [keep.tile([P, HO], F32, name="result%d%d" % (h, n)) for n in range(2)]
            nc.scalar.copy(result[0][:], out_banks[h, 0][:, 0:HO])
            nc.scalar.dma_start(out[0:P, h * HO : (h + 1) * HO], result[0][:])
            nc.vector.tensor_copy(result[1][:], out_banks[h, 1][:, 0:HO])
            nc.sync.dma_start(out[P : 2 * P, h * HO : (h + 1) * HO], result[1][:])
